import numpy as np
import ml_dtypes

BF16 = ml_dtypes.bfloat16


def bf(x):
    return np.asarray(x, np.float32).astype(BF16)


def f32(x):
    return np.asarray(x, np.float32)


def f64(x):
    return np.asarray(x).astype(np.float64)


def striped(idx):
    return np.tile(idx.reshape(-1, 16).T, (8, 1))


def rows(idx, k):
    return np.tile(idx, (k, 1))


def look(tab, idx):
    return np.take_along_axis(f64(tab), rows(idx, len(tab)), axis=1)


K, S, V, N = 256, 2048, 1024, 1024


def setup_inputs():
    return {"tab": f32(np.random.standard_normal((2, K, S))), "offs": striped(np.random.permutation(S)[:N])}


def reference(tab, offs):
    idx = offs[:16].T.reshape(-1)
    x = ((look(tab[0], idx) - 0.125) * 1.5) * (np.tanh(look(tab[1], idx)))
    return x

@@ -1,0 +1,37 @@
+import concourse.mybir as mybir
+
+F32, U16 = mybir.dt.float32, mybir.dt.uint16
+ALU = mybir.AluOpType
+TANH = mybir.ActivationFunctionType.Tanh
+
+P = 128
+SHIFT, SCALE = 0.125, 1.5
+
+
+def tile_lookup_vg_nrmtanh_out_kernel(tc, tab, offs, out):
+    nc = tc.nc
+    rows, places = tab.shape[1], tab.shape[2]
+    count = out.shape[1]
+    with (
+        tc.tile_pool(name="held", bufs=1) as held,
+        tc.tile_pool(name="windows", bufs=2) as windows,
+        tc.tile_pool(name="results", bufs=2) as results,
+    ):
+        offsets = held.tile([P, count // 16], U16, name="offsets")
+        nc.sync.dma_start(offsets[:], offs)
+        for block in range(rows // P):
+            r0 = block * P
+            values = windows.tile([P, places], F32, name="values")
+            gates = windows.tile([P, places], F32, name="gates")
+            nc.sync.dma_start(values[:], tab[0, r0 : r0 + P, :])
+            nc.sync.dma_start(gates[:], tab[1, r0 : r0 + P, :])
+
+            scaled = results.tile([P, count], F32, name="scaled")
+            opened = results.tile([P, count], F32, name="opened")
+            product = results.tile([P, count], F32, name="product")
+            nc.vector.tensor_scalar(
+                scaled[:], values[:].indirect(offsets[:]), SHIFT, SCALE, ALU.subtract, ALU.mult
+            )
+            nc.scalar.activation(opened[:], gates[:].indirect(offsets[:]), TANH)
+            nc.vector.tensor_tensor(product[:], scaled[:], opened[:], ALU.mult)
+            nc.sync.dma_start(out[r0 : r0 + P, :], product[:])

@@ -5,6 +5,7 @@ ALU = mybir.AluOpType
 TANH = mybir.ActivationFunctionType.Tanh
 
 P = 128
+PIECE = 256
 SHIFT, SCALE = 0.125, 1.5
 
 
@@ -27,11 +28,16 @@ def tile_lookup_vg_nrmtanh_out_kernel(tc, tab, offs, out):
             nc.sync.dma_start(gates[:], tab[1, r0 : r0 + P, :])
 
             scaled = results.tile([P, count], F32, name="scaled")
+            for a in range(0, count, PIECE):
+                piece = offsets[:, a // 16 : (a + PIECE) // 16]
+                nc.vector.tensor_scalar(
+                    scaled[:, a : a + PIECE], values[:].indirect(piece), SHIFT, SCALE, ALU.subtract, ALU.mult
+                )
             opened = results.tile([P, count], F32, name="opened")
             product = results.tile([P, count], F32, name="product")
-            nc.vector.tensor_scalar(
-                scaled[:], values[:].indirect(offsets[:]), SHIFT, SCALE, ALU.subtract, ALU.mult
-            )
-            nc.scalar.activation(opened[:], gates[:].indirect(offsets[:]), TANH)
-            nc.vector.tensor_tensor(product[:], scaled[:], opened[:], ALU.mult)
-            nc.sync.dma_start(out[r0 : r0 + P, :], product[:])
+            for a in range(0, count, PIECE):
+                piece = offsets[:, a // 16 : (a + PIECE) // 16]
+                now = slice(a, a + PIECE)
+                nc.scalar.activation(opened[:, now], gates[:].indirect(piece), TANH)
+                nc.vector.tensor_tensor(product[:, now], scaled[:, now], opened[:, now], ALU.mult)
+                nc.sync.dma_start(out[r0 : r0 + P, now], product[:, now])

@@ -18,6 +18,11 @@ def tile_lookup_vg_nrmtanh_out_kernel(tc, tab, offs, out):
         tc.tile_pool(name="windows", bufs=2) as windows,
         tc.tile_pool(name="results", bufs=2) as results,
     ):
+        zeros = held.tile([P, 1], F32, name="zeros")
+        warm = held.tile([P, 1], F32, name="warm")
+        nc.vector.memset(zeros[:], 0.0)
+        nc.scalar.activation(warm[:], zeros[:], TANH)
+
         offsets = held.tile([P, count // 16], U16, name="offsets")
         nc.sync.dma_start(offsets[:], offs)
         for block in range(rows // P):

import concourse.mybir as mybir

F32, U16 = mybir.dt.float32, mybir.dt.uint16
ALU = mybir.AluOpType
TANH = mybir.ActivationFunctionType.Tanh

P = 128
PIECE = 256
SHIFT, SCALE = 0.125, 1.5


def tile_lookup_vg_nrmtanh_out_kernel(tc, tab, offs, out):
    nc = tc.nc
    rows, places = tab.shape[1], tab.shape[2]
    count = out.shape[1]
    with (
        tc.tile_pool(name="held", bufs=1) as held,
        tc.tile_pool(name="windows", bufs=2) as windows,
        tc.tile_pool(name="results", bufs=2) as results,
    ):
        zeros = held.tile([P, 1], F32, name="zeros")
        warm = held.tile([P, 1], F32, name="warm")
        nc.vector.memset(zeros[:], 0.0)
        nc.scalar.activation(warm[:], zeros[:], TANH)

        offsets = held.tile([P, count // 16], U16, name="offsets")
        nc.sync.dma_start(offsets[:], offs)
        for block in range(rows // P):
            r0 = block * P
            values = windows.tile([P, places], F32, name="values")
            gates = windows.tile([P, places], F32, name="gates")
            nc.sync.dma_start(values[:], tab[0, r0 : r0 + P, :])
            nc.sync.dma_start(gates[:], tab[1, r0 : r0 + P, :])

            scaled = results.tile([P, count], F32, name="scaled")
            for a in range(0, count, PIECE):
                piece = offsets[:, a // 16 : (a + PIECE) // 16]
                nc.vector.tensor_scalar(
                    scaled[:, a : a + PIECE], values[:].indirect(piece), SHIFT, SCALE, ALU.subtract, ALU.mult
                )
            opened = results.tile([P, count], F32, name="opened")
            product = results.tile([P, count], F32, name="product")
            for a in range(0, count, PIECE):
                piece = offsets[:, a // 16 : (a + PIECE) // 16]
                now = slice(a, a + PIECE)
                nc.scalar.activation(opened[:, now], gates[:].indirect(piece), TANH)
                nc.vector.tensor_tensor(product[:, now], scaled[:, now], opened[:, now], ALU.mult)
                nc.sync.dma_start(out[r0 : r0 + P, now], product[:, now])
